import numpy as np
import ml_dtypes


def mxq(x, axis, fmt="e4m3"):
    dtype, down = {"e4m3": (ml_dtypes.float8_e4m3fn, 7), "e5m2": (ml_dtypes.float8_e5m2, 14)}[fmt]
    v = np.moveaxis(np.asarray(x, np.float32).astype(ml_dtypes.bfloat16).astype(np.float64), axis, -1)
    blocks = v.reshape(v.shape[:-1] + (-1, 32))
    amax = np.abs(blocks).max(-1, keepdims=True)
    byte = np.maximum(np.where(amax > 0, np.frexp(amax)[1] - 1 + 127, 0) - down, 1)
    scale = np.exp2(byte - 127.0)
    codes = (blocks / scale).astype(np.float32).astype(dtype).astype(np.float64)
    return np.moveaxis((codes * scale).reshape(v.shape), -1, axis)


WIDE = False


def mx_kscale(k):
    if not WIDE:
        return np.ones(k)
    levels = np.array([10, -10, 5, -5, 0])
    if k % 512:
        return np.exp2(np.random.permutation(np.resize(levels, k // 32))).repeat(32)
    a = np.empty((k // 512, 16))
    for p in range(k // 512):
        a[p, :8] = np.random.permutation(np.resize(levels, 8))
        for g in range(8):
            far = levels[np.abs(levels - a[p, g]) >= 10]
            a[p, g + 8] = far[np.random.randint(len(far))]
    return np.exp2(a.ravel()).repeat(32)


BF16 = ml_dtypes.bfloat16


def bf(x):
    return np.asarray(x, np.float32).astype(BF16)


def f64(x):
    return np.asarray(x).astype(np.float64)


E2M1 = np.array([0.0, 0.5, 1.0, 1.5, 2.0, 3.0, 4.0, 6.0, -0.0, -0.5, -1.0, -1.5, -2.0, -3.0, -4.0, -6.0])


def pack_weight(w, fmt):
    k, n = w.shape
    w = f64(bf(w)).reshape(k // 32, 32, n)
    amax = np.abs(w).max(1)
    if fmt == "e4m3":
        byte = np.frexp(amax)[1] - 1 + 127 - 7
    else:
        mant, ex = np.frexp(amax / 6.0)
        byte = np.where(mant > 0.5, ex, ex - 1) + 127
    byte = np.clip(np.where(amax > 0, byte, 1), 1, 254)
    scaled = (w * np.exp2(127.0 - byte)[:, None, :]).reshape(k, n).astype(np.float32)
    by_word = np.ascontiguousarray(scaled.reshape(k // 512, 128, 4, n).transpose(0, 1, 3, 2))
    if fmt == "e4m3":
        words = by_word.astype(ml_dtypes.float8_e4m3fn).view(np.uint8)
    else:
        c = by_word.astype(ml_dtypes.float4_e2m1fn).view(np.uint8) & 0xF
        words = c[..., 0::2] | (c[..., 1::2] << 4)
    return np.ascontiguousarray(words), np.ascontiguousarray(byte.astype(np.uint8).reshape(k // 512, 16, n))


def unpack_weight(words, scales, fmt):
    g, p, n, _ = words.shape
    if fmt == "e4m3":
        vals = np.ascontiguousarray(words).view(ml_dtypes.float8_e4m3fn).astype(np.float64)
    else:
        nib = np.empty((g, p, n, 4), np.uint8)
        nib[..., 0::2] = words & 0xF
        nib[..., 1::2] = words >> 4
        vals = E2M1[nib]
    vals = vals * np.repeat(np.exp2(scales.astype(np.float64) - 127.0), 8, axis=1)[..., None]
    return vals.transpose(0, 1, 3, 2).reshape(g * 512, n)
def pack4(w):
    words, scales = pack_weight(w, "e2m1")
    return words.reshape(words.shape[0], 128, -1), scales


def unpack4(words, scales):
    return unpack_weight(words.reshape(words.shape[0], 128, -1, 2), scales, "e2m1")


def planes(Y):
    n, m = Y.shape
    b = f64(bf(Y)).reshape(n // 32, 32, m)
    amax = np.abs(b).max(1)
    byte = np.clip(np.where(amax > 0, np.frexp(amax)[1] - 1 + 127 - 7, 1), 1, 254)
    codes = (b * np.exp2(127.0 - byte)[:, None, :]).reshape(n, m).astype(np.float32).astype(ml_dtypes.float8_e4m3fn).view(np.uint8)
    words = codes.reshape(n // 512, 128, 4, m).transpose(0, 1, 3, 2)
    return np.ascontiguousarray(words), np.ascontiguousarray(byte.astype(np.uint8).reshape(n // 512, 16, m))


N = 1024
BETA = 0.5

def setup_inputs():
    s, t = mx_kscale(N), mx_kscale(N)
    a_words, a_scales = pack4(np.random.randn(N, N) / np.sqrt(N) * s[:, None])
    AT = unpack4(a_words, a_scales) / s[:, None]
    m_words, m_scales = pack4((0.5 * AT + 0.1 * np.random.randn(N, N)) / s[:, None])
    v = f64(bf(3.0 * np.exp(0.3 * np.random.randn(N))))
    va = bf((v / t)[:, None] * AT.T)
    step = np.exp(0.8 * np.random.randn(N))
    d_prev = bf(step[:, None] * np.random.randn(N, N))
    return {"a_words": a_words, "a_scales": a_scales, "m_words": m_words, "m_scales": m_scales,
            "va": va, "v": bf(v * t), "step": bf(step), "d_prev": d_prev}

def reference(a_words, a_scales, m_words, m_scales, va, v, step, d_prev):
    AT = unpack4(a_words, a_scales)
    M = unpack4(m_words, m_scales)
    AM = AT.T @ M
    R = f64(v)[:, None] * (np.eye(N) - AM)
    G = mxq(f64(va), 0, "e4m3").T @ mxq(R, 0, "e4m3")
    y = f64(step)[:, None] * G + BETA * f64(d_prev)
    Y = y.reshape(N, N)
    words, scales = planes(Y)
    return y, words, scales

@@ -1,0 +1,384 @@
+from contextlib import ExitStack
+
+import concourse.mybir as mybir
+from concourse.masks import make_identity
+
+N = 1024
+FLOPS = 2 * 2 * N * N * N
+
+F32 = mybir.dt.float32
+BF16 = mybir.dt.bfloat16
+I32 = mybir.dt.int32
+U32 = mybir.dt.uint32
+U8 = mybir.dt.uint8
+FP8X4 = mybir.dt.float8_e4m3fn_x4
+FP4X4 = mybir.dt.float4_e2m1fn_x4
+COPY = mybir.ActivationFunctionType.Copy
+MULT = mybir.AluOpType.mult
+ADD = mybir.AluOpType.add
+
+P = 128
+PACK = 4
+HALF = 512
+GROUPS = N // HALF
+BANKS = 8
+BETA = 0.5
+
+
+def tile_approximate_inverse_descent_directio_k5_kernel(
+    tc, a_words, a_scales, m_words, m_scales, va, v, step, d_prev, out_0, out_1, out_2
+):
+    nc = tc.nc
+    with ExitStack() as ctx:
+        keep = ctx.enter_context(tc.tile_pool(name="keep", bufs=1))
+        psum = ctx.enter_context(tc.psum_pool(name="psum", bufs=1))
+        ctx.enter_context(tc.manual_schedule())
+
+        def sb(name, shape, dtype):
+            return keep.tile(shape, dtype, name=name, align_bytes=64)
+
+        bank_count = [0]
+
+        def new_bank(shape, dtype):
+            k = bank_count[0] % BANKS
+            bank_count[0] += 1
+            return psum.tile(shape, dtype, name="bank%d" % k)
+
+        ident = sb("ident", [P, P], BF16)
+        neg_ident = sb("neg_ident", [P, P], BF16)
+        v_rows = sb("v_rows", [P, GROUPS, P], BF16)
+        neg_v = sb("neg_v", [P, GROUPS, PACK], F32)
+        v_diag = sb("v_diag", [P, GROUPS, PACK, P], BF16)
+        step_sb = sb("step_sb", [P, GROUPS, PACK], BF16)
+        a_raw = sb("a_raw", [P, GROUPS, 2 * N], U8)
+        a_raw_sc = sb("a_raw_sc", [P, GROUPS, N], U8)
+        a_st = sb("a_st", [P, GROUPS, 2 * N], U8)
+        a_sc = sb("a_sc", [P, GROUPS, N], U8)
+        m_mv = sb("m_mv", [P, GROUPS, 2 * N], U8)
+        m_sc = sb("m_sc", [P, GROUPS, N], U8)
+        va_raw = [sb("va_raw%d" % g, [P, PACK, N], BF16) for g in range(GROUPS)]
+        va_il = [[sb("va_il%d%d" % (g, h), [P, PACK * HALF], BF16) for h in range(GROUPS)] for g in range(GROUPS)]
+        va_codes = sb("va_codes", [P, GROUPS, N], U32)
+        va_sc = sb("va_sc", [P, GROUPS, N], U8)
+        r_rows = [sb("r_rows%d" % g, [P, PACK, N], BF16) for g in range(GROUPS)]
+        r_il = [sb("r_il%d" % g, [P, N * PACK], BF16) for g in range(GROUPS)]
+        r_codes = sb("r_codes", [P, GROUPS, N], U32)
+        r_sc = sb("r_sc", [P, GROUPS, N], U8)
+        d_raw = [sb("d_raw%d" % g, [P, PACK, N], BF16) for g in range(GROUPS)]
+        d_half = [sb("d_half%d" % g, [P, PACK, N], BF16) for g in range(GROUPS)]
+        y = [sb("y%d" % g, [P, PACK, N], F32) for g in range(GROUPS)]
+        y_il = [sb("y_il%d" % g, [P, N * PACK], BF16) for g in range(GROUPS)]
+        y_codes = sb("y_codes", [P, GROUPS, N], U32)
+        y_sc = sb("y_sc", [P, GROUPS, N], U8)
+
+        def copy_on(engine, out, in_):
+            if engine == "V":
+                nc.vector.tensor_copy(out=out, in_=in_)
+            else:
+                nc.scalar.copy(out=out, in_=in_)
+
+        def load_va(queue, g, h):
+            cols = slice(h * HALF, (h + 1) * HALF)
+            rows = va[g * HALF : (g + 1) * HALF, cols].rearrange("(m t e) c -> e m t c", t=PACK, e=PACK)
+            for e in range(PACK):
+                queue.dma_start(out=va_raw[g][e:P:PACK, :, cols], in_=rows[e])
+
+        def load_scale(queue, plane, scales, q):
+            queue.dma_start(
+                out=plane[32 * q : 32 * q + 4, :, :].bitcast(I32),
+                in_=scales[:, 4 * q : 4 * q + 4, :].rearrange("g r n -> r g n").bitcast(I32),
+            )
+
+        def load_d(queue, g, j0, width):
+            queue.dma_start(
+                out=d_raw[g][:, :, j0 : j0 + width],
+                in_=d_prev[g * HALF : (g + 1) * HALF, j0 : j0 + width].rearrange("(p t) n -> p t n", t=PACK),
+            )
+
+        def clear(plane):
+            nc.vector.memset(plane[:].bitcast(I32), 0)
+
+        def identity():
+            make_identity(nc, ident[:])
+
+        def neg_identity():
+            nc.scalar.activation(out=neg_ident[:], in_=ident[:], func=COPY, scale=-1.0)
+
+        def load_a(queue):
+            queue.dma_start(out=a_raw[:].bitcast(I32), in_=a_words.rearrange("g p n -> p g n").bitcast(I32))
+
+        def load_m(queue, j0, width):
+            cols = slice(2 * j0, 2 * (j0 + width))
+            queue.dma_start(
+                out=m_mv[:, :, cols].bitcast(I32), in_=m_words[:, :, cols].rearrange("g p n -> p g n").bitcast(I32)
+            )
+
+        def load_v(queue):
+            queue.dma_start(
+                out=v_rows[0:PACK, :, :].rearrange("t g (m e) -> t (g m) e", e=PACK),
+                in_=v.rearrange("(m t e) -> t m e", t=PACK, e=PACK),
+            )
+
+        def load_step(queue):
+            queue.dma_start(out=step_sb[:], in_=step.rearrange("(g p t) -> p g t", p=P, t=PACK))
+
+        def permute_a(g):
+            for kg in range(GROUPS):
+                cols = slice(2 * g * HALF, 2 * (g + 1) * HALF)
+                nc.vector.tensor_copy(
+                    out=a_st[:, kg, cols].bitcast(I32).rearrange("p (t m w) -> p t m w", t=PACK, w=2),
+                    in_=a_raw[:, kg, cols].bitcast(I32).rearrange("p (m t w) -> p t m w", t=PACK, w=2),
+                )
+            cols = slice(g * HALF, (g + 1) * HALF)
+            nc.vector.tensor_copy(
+                out=a_sc[:, :, cols].bitcast(I32).rearrange("p k (t m) -> p k t m", t=PACK),
+                in_=a_raw_sc[:, :, cols].bitcast(I32).rearrange("p k (m t) -> p k t m", t=PACK),
+            )
+
+        def prepare_v():
+            bank = new_bank([P, GROUPS, P], BF16)
+            for g in range(GROUPS):
+                nc.tensor.transpose(bank[:, g, :], v_rows[:, g, :], ident[:])
+            nc.scalar.activation(out=neg_v[:], in_=bank[:, :, 0:PACK], func=COPY, scale=-1.0)
+
+        def make_v_diag(g):
+            for t in range(PACK):
+                nc.scalar.activation(
+                    out=v_diag[:, g, t, :], in_=neg_ident[:], func=COPY, scale=neg_v[:, g, t : t + 1]
+                )
+
+        def interleave_va(engine, g, h, part=None):
+            cols = slice(h * HALF, (h + 1) * HALF)
+            us = slice(0, PACK) if part is None else slice(2 * part, 2 * part + 2)
+            copy_on(
+                engine,
+                va_il[g][h][:].rearrange("p (u a b t) -> p u a t b", u=PACK, b=4, t=PACK)[:, us],
+                va_raw[g][:, :, cols].rearrange("p t (a b u) -> p u a t b", u=PACK, b=4)[:, us],
+            )
+
+        def quantize_va(g, h):
+            cols = slice(h * HALF, (h + 1) * HALF)
+            nc.vector.quantize_mx(out=va_codes[:, g, cols].bitcast(FP8X4), scales=va_sc[:, g, cols], in_=va_il[g][h][:])
+
+        am_banks = {}
+
+        def multiply_am(g, j0, width, t):
+            bank = new_bank([P, width], F32)
+            am_banks[g, j0, t] = bank
+            i0 = g * HALF + t * P
+            for kg in range(GROUPS):
+                nc.tensor.matmul_mx(
+                    out=bank[:],
+                    lhsT=a_st[:, kg, 2 * i0 : 2 * (i0 + P)].bitcast(FP4X4),
+                    lhsT_scale=a_sc[:, kg, i0 : i0 + P],
+                    rhs=m_mv[:, kg, 2 * j0 : 2 * (j0 + width)].bitcast(FP4X4),
+                    rhs_scale=m_sc[:, kg, j0 : j0 + width],
+                    start=(kg == 0),
+                    stop=(kg == GROUPS - 1),
+                )
+
+        def residual(g, j0, width, t):
+            bank = am_banks[g, j0, t][:].rearrange("p (m u e) -> p u m e", u=PACK, e=PACK)
+            row = r_rows[g][:, t, j0 : j0 + width].rearrange("p (u m e) -> p u m e", u=PACK, e=PACK)
+            spans = [(0, t), (t + 1, PACK)] if g == j0 // HALF else [(0, PACK)]
+            for u0, u1 in spans:
+                if u1 > u0:
+                    nc.scalar.activation(
+                        out=row[:, u0:u1], in_=bank[:, u0:u1], func=COPY, scale=neg_v[:, g, t : t + 1]
+                    )
+
+        def diag(j0, width):
+            g = j0 // HALF
+            p0 = (j0 - g * HALF) // PACK
+            for t in range(PACK):
+                bank = am_banks[g, j0, t][:].rearrange("p (m u e) -> p u m e", u=PACK, e=PACK)
+                row = r_rows[g][:, t, j0 : j0 + width].rearrange("p (u m e) -> p u m e", u=PACK, e=PACK)
+                nc.vector.scalar_tensor_tensor(
+                    out=row[:, t],
+                    in0=bank[:, t],
+                    scalar=neg_v[:, g, t : t + 1],
+                    in1=v_diag[:, g, t, p0 : p0 + width // PACK].rearrange("p (m e) -> p m e", e=PACK),
+                    op0=MULT,
+                    op1=ADD,
+                )
+
+        def interleave_r(engine, g, j0, width):
+            copy_on(
+                engine,
+                r_il[g][:, PACK * j0 : PACK * (j0 + width)].rearrange(
+                    "p (m u e t) -> p u m t e", u=PACK, e=PACK, t=PACK
+                ),
+                r_rows[g][:, :, j0 : j0 + width].rearrange("p t (u m e) -> p u m t e", u=PACK, e=PACK),
+            )
+
+        def quantize_r(g, j0, width):
+            nc.vector.quantize_mx(
+                out=r_codes[:, g, j0 : j0 + width].bitcast(FP8X4),
+                scales=r_sc[:, g, j0 : j0 + width],
+                in_=r_il[g][:, PACK * j0 : PACK * (j0 + width)],
+            )
+
+        def halve_d(g, j0, width):
+            cols = slice(j0, j0 + width)
+            nc.vector.tensor_scalar(
+                out=d_half[g][:, :, cols], in0=d_raw[g][:, :, cols], scalar1=BETA, scalar2=None, op0=MULT
+            )
+
+        g_banks = {}
+
+        def multiply_g(g, j0, width, t):
+            bank = new_bank([P, width], F32)
+            g_banks[g, j0, t] = bank
+            c0 = g * HALF + t * P
+            for kg in range(GROUPS):
+                nc.tensor.matmul_mx(
+                    out=bank[:],
+                    lhsT=va_codes[:, kg, c0 : c0 + P].bitcast(FP8X4),
+                    lhsT_scale=va_sc[:, kg, c0 : c0 + P],
+                    rhs=r_codes[:, kg, j0 : j0 + width].bitcast(FP8X4),
+                    rhs_scale=r_sc[:, kg, j0 : j0 + width],
+                    start=(kg == 0),
+                    stop=(kg == GROUPS - 1),
+                )
+
+        def direction(g, j0, width, t):
+            nc.vector.scalar_tensor_tensor(
+                out=y[g][:, t, j0 : j0 + width],
+                in0=g_banks[g, j0, t][:],
+                scalar=step_sb[:, g, t : t + 1],
+                in1=d_half[g][:, t, j0 : j0 + width],
+                op0=MULT,
+                op1=ADD,
+            )
+
+        def store_y(g, j0, width, t0, t1):
+            rows = out_0[g * HALF : (g + 1) * HALF, j0 : j0 + width].rearrange("(p t) n -> p t n", t=PACK)
+            nc.sync.dma_start(out=rows[:, t0:t1, :], in_=y[g][:, t0:t1, j0 : j0 + width])
+
+        def interleave_y(engine, g, j0, width):
+            copy_on(
+                engine,
+                y_il[g][:, PACK * j0 : PACK * (j0 + width)].rearrange("p (a b t) -> p a t b", b=4, t=PACK),
+                y[g][:, :, j0 : j0 + width].rearrange("p t (a b) -> p a t b", b=4),
+            )
+
+        def quantize_y(g, j0, width):
+            nc.vector.quantize_mx(
+                out=y_codes[:, g, j0 : j0 + width].bitcast(FP8X4),
+                scales=y_sc[:, g, j0 : j0 + width],
+                in_=y_il[g][:, PACK * j0 : PACK * (j0 + width)],
+            )
+
+        def store_codes(g, j0, width):
+            nc.sync.dma_start(
+                out=out_1[g].rearrange("p n t -> p (n t)")[:, PACK * j0 : PACK * (j0 + width)].bitcast(I32),
+                in_=y_codes[:, g, j0 : j0 + width].bitcast(I32),
+            )
+
+        def store_scales(queue):
+            for q in range(4):
+                queue.dma_start(
+                    out=out_2[:, 4 * q : 4 * q + 4, :].rearrange("g r n -> r g n").bitcast(I32),
+                    in_=y_sc[32 * q : 32 * q + 4, :, :].bitcast(I32),
+                )
+
+        def stage1(g, j0, width):
+            for t in range(PACK):
+                multiply_am(g, j0, width, t)
+                residual(g, j0, width, t)
+
+        def stage2_mm(g, j0, width):
+            for t in range(PACK):
+                multiply_g(g, j0, width, t)
+
+        def stage2_out(g, j0, width, stores):
+            per_store = PACK // stores
+            for t in range(PACK):
+                direction(g, j0, width, t)
+                if (t + 1) % per_store == 0:
+                    store_y(g, j0, width, t + 1 - per_store, t + 1)
+
+        clear(a_raw_sc)
+        clear(m_sc)
+        clear(v_rows)
+        load_va(nc.scalar, 0, 0)
+        identity()
+        load_scale(nc.sync, a_raw_sc, a_scales, 0)
+        load_scale(nc.sync, a_raw_sc, a_scales, 1)
+        load_scale(nc.sync, a_raw_sc, a_scales, 2)
+        load_scale(nc.sync, a_raw_sc, a_scales, 3)
+        load_scale(nc.gpsimd, m_sc, m_scales, 0)
+        load_scale(nc.gpsimd, m_sc, m_scales, 1)
+        load_scale(nc.gpsimd, m_sc, m_scales, 2)
+        load_scale(nc.gpsimd, m_sc, m_scales, 3)
+        neg_identity()
+        load_a(nc.sync)
+        load_v(nc.sync)
+        load_m(nc.sync, 0, 512)
+        load_va(nc.sync, 1, 0)
+        load_step(nc.sync)
+        load_va(nc.sync, 0, 1)
+        load_va(nc.sync, 1, 1)
+        load_m(nc.sync, 512, 512)
+        load_d(nc.sync, 0, 0, 512)
+        load_d(nc.sync, 1, 0, 512)
+        load_d(nc.sync, 0, 512, 512)
+        load_d(nc.sync, 1, 512, 512)
+        interleave_va("V", 0, 0, 0)
+        interleave_va("S", 0, 0, 1)
+        prepare_v()
+        make_v_diag(0)
+        make_v_diag(1)
+        quantize_va(0, 0)
+        permute_a(0)
+        permute_a(1)
+        stage1(0, 0, 512)
+        interleave_va("V", 1, 0)
+        interleave_va("V", 0, 1)
+        quantize_va(1, 0)
+        diag(0, 512)
+        stage1(1, 0, 512)
+        interleave_va("V", 1, 1)
+        quantize_va(0, 1)
+        interleave_r("V", 0, 0, 512)
+        stage1(0, 512, 512)
+        quantize_va(1, 1)
+        interleave_r("V", 1, 0, 512)
+        halve_d(0, 0, 512)
+        quantize_r(0, 0, 512)
+        stage1(1, 512, 512)
+        quantize_r(1, 0, 512)
+        stage2_mm(0, 0, 512)
+        interleave_r("S", 0, 512, 512)
+        halve_d(1, 0, 512)
+        diag(512, 512)
+        stage2_out(0, 0, 512, 2)
+        stage2_mm(1, 0, 512)
+        quantize_r(0, 512, 512)
+        interleave_r("S", 1, 512, 512)
+        stage2_out(1, 0, 512, 2)
+        interleave_y("S", 0, 0, 512)
+        quantize_r(1, 512, 512)
+        halve_d(0, 512, 512)
+        interleave_y("S", 1, 0, 512)
+        halve_d(1, 512, 256)
+        halve_d(1, 768, 256)
+        stage2_mm(0, 512, 512)
+        quantize_y(0, 0, 512)
+        store_codes(0, 0, 512)
+        stage2_out(0, 512, 512, 2)
+        quantize_y(1, 0, 512)
+        store_codes(1, 0, 512)
+        stage2_mm(1, 512, 256)
+        stage2_mm(1, 768, 256)
+        stage2_out(1, 512, 256, 1)
+        interleave_y("S", 0, 512, 512)
+        stage2_out(1, 768, 256, 1)
+        interleave_y("S", 1, 512, 256)
+        quantize_y(0, 512, 512)
+        interleave_y("V", 1, 768, 256)
+        quantize_y(1, 512, 256)
+        store_codes(0, 512, 512)
+        quantize_y(1, 768, 256)
+        store_scales(nc.scalar)
+        store_codes(1, 512, 512)

@@ -52,21 +52,21 @@ def tile_approximate_inverse_descent_directio_k5_kernel(
         step_sb = sb("step_sb", [P, GROUPS, PACK], BF16)
         a_raw = sb("a_raw", [P, GROUPS, 2 * N], U8)
         a_raw_sc = sb("a_raw_sc", [P, GROUPS, N], U8)
-        a_st = sb("a_st", [P, GROUPS, 2 * N], U8)
-        a_sc = sb("a_sc", [P, GROUPS, N], U8)
-        m_mv = sb("m_mv", [P, GROUPS, 2 * N], U8)
+        a_st = [sb("a_st%d" % g, [P, GROUPS, 2 * HALF], U8) for g in range(GROUPS)]
+        a_sc = [sb("a_sc%d" % g, [P, GROUPS, HALF], U8) for g in range(GROUPS)]
+        m_mv = [sb("m_mv%d" % h, [P, GROUPS, 2 * HALF], U8) for h in range(GROUPS)]
         m_sc = sb("m_sc", [P, GROUPS, N], U8)
-        va_raw = [sb("va_raw%d" % g, [P, PACK, N], BF16) for g in range(GROUPS)]
+        va_raw = [[sb("va_raw%d%d" % (g, h), [P, PACK, HALF], BF16) for h in range(GROUPS)] for g in range(GROUPS)]
         va_il = [[sb("va_il%d%d" % (g, h), [P, PACK * HALF], BF16) for h in range(GROUPS)] for g in range(GROUPS)]
         va_codes = sb("va_codes", [P, GROUPS, N], U32)
         va_sc = sb("va_sc", [P, GROUPS, N], U8)
-        r_rows = [sb("r_rows%d" % g, [P, PACK, N], BF16) for g in range(GROUPS)]
+        r_rows = {}
         r_il = [sb("r_il%d" % g, [P, N * PACK], BF16) for g in range(GROUPS)]
         r_codes = sb("r_codes", [P, GROUPS, N], U32)
         r_sc = sb("r_sc", [P, GROUPS, N], U8)
         d_raw = [sb("d_raw%d" % g, [P, PACK, N], BF16) for g in range(GROUPS)]
         d_half = [sb("d_half%d" % g, [P, PACK, N], BF16) for g in range(GROUPS)]
-        y = [sb("y%d" % g, [P, PACK, N], F32) for g in range(GROUPS)]
+        y = {}
         y_il = [sb("y_il%d" % g, [P, N * PACK], BF16) for g in range(GROUPS)]
         y_codes = sb("y_codes", [P, GROUPS, N], U32)
         y_sc = sb("y_sc", [P, GROUPS, N], U8)
@@ -81,7 +81,7 @@ def tile_approximate_inverse_descent_directio_k5_kernel(
             cols = slice(h * HALF, (h + 1) * HALF)
             rows = va[g * HALF : (g + 1) * HALF, cols].rearrange("(m t e) c -> e m t c", t=PACK, e=PACK)
             for e in range(PACK):
-                queue.dma_start(out=va_raw[g][e:P:PACK, :, cols], in_=rows[e])
+                queue.dma_start(out=va_raw[g][h][e:P:PACK, :, :], in_=rows[e])
 
         def load_scale(queue, plane, scales, q):
             queue.dma_start(
@@ -89,10 +89,9 @@ def tile_approximate_inverse_descent_directio_k5_kernel(
                 in_=scales[:, 4 * q : 4 * q + 4, :].rearrange("g r n -> r g n").bitcast(I32),
             )
 
-        def load_d(queue, g, j0, width):
+        def load_d(queue, g):
             queue.dma_start(
-                out=d_raw[g][:, :, j0 : j0 + width],
-                in_=d_prev[g * HALF : (g + 1) * HALF, j0 : j0 + width].rearrange("(p t) n -> p t n", t=PACK),
+                out=d_raw[g][:], in_=d_prev[g * HALF : (g + 1) * HALF, :].rearrange("(p t) n -> p t n", t=PACK)
             )
 
         def clear(plane):
@@ -110,7 +109,7 @@ def tile_approximate_inverse_descent_directio_k5_kernel(
         def load_m(queue, j0, width):
             cols = slice(2 * j0, 2 * (j0 + width))
             queue.dma_start(
-                out=m_mv[:, :, cols].bitcast(I32), in_=m_words[:, :, cols].rearrange("g p n -> p g n").bitcast(I32)
+                out=m_mv[j0 // HALF][:].bitcast(I32), in_=m_words[:, :, cols].rearrange("g p n -> p g n").bitcast(I32)
             )
 
         def load_v(queue):
@@ -123,15 +122,15 @@ def tile_approximate_inverse_descent_directio_k5_kernel(
             queue.dma_start(out=step_sb[:], in_=step.rearrange("(g p t) -> p g t", p=P, t=PACK))
 
         def permute_a(g):
-            for kg in range(GROUPS):
-                cols = slice(2 * g * HALF, 2 * (g + 1) * HALF)
-                nc.vector.tensor_copy(
-                    out=a_st[:, kg, cols].bitcast(I32).rearrange("p (t m w) -> p t m w", t=PACK, w=2),
-                    in_=a_raw[:, kg, cols].bitcast(I32).rearrange("p (m t w) -> p t m w", t=PACK, w=2),
-                )
+            nc.vector.tensor_copy(
+                out=a_st[g][:].bitcast(I32).rearrange("p k (t m w) -> p k t m w", t=PACK, w=2),
+                in_=a_raw[:, :, 2 * g * HALF : 2 * (g + 1) * HALF]
+                .bitcast(I32)
+                .rearrange("p k (m t w) -> p k t m w", t=PACK, w=2),
+            )
             cols = slice(g * HALF, (g + 1) * HALF)
             nc.vector.tensor_copy(
-                out=a_sc[:, :, cols].bitcast(I32).rearrange("p k (t m) -> p k t m", t=PACK),
+                out=a_sc[g][:].bitcast(I32).rearrange("p k (t m) -> p k t m", t=PACK),
                 in_=a_raw_sc[:, :, cols].bitcast(I32).rearrange("p k (m t) -> p k t m", t=PACK),
             )
 
@@ -141,19 +140,23 @@ def tile_approximate_inverse_descent_directio_k5_kernel(
                 nc.tensor.transpose(bank[:, g, :], v_rows[:, g, :], ident[:])
             nc.scalar.activation(out=neg_v[:], in_=bank[:, :, 0:PACK], func=COPY, scale=-1.0)
 
-        def make_v_diag(g):
+        def make_v_diag(engine, g):
             for t in range(PACK):
-                nc.scalar.activation(
-                    out=v_diag[:, g, t, :], in_=neg_ident[:], func=COPY, scale=neg_v[:, g, t : t + 1]
-                )
+                if engine == "V":
+                    nc.vector.tensor_scalar(
+                        out=v_diag[:, g, t, :], in0=neg_ident[:], scalar1=neg_v[:, g, t : t + 1], scalar2=None, op0=MULT
+                    )
+                else:
+                    nc.scalar.activation(
+                        out=v_diag[:, g, t, :], in_=neg_ident[:], func=COPY, scale=neg_v[:, g, t : t + 1]
+                    )
 
         def interleave_va(engine, g, h, part=None):
-            cols = slice(h * HALF, (h + 1) * HALF)
             us = slice(0, PACK) if part is None else slice(2 * part, 2 * part + 2)
             copy_on(
                 engine,
                 va_il[g][h][:].rearrange("p (u a b t) -> p u a t b", u=PACK, b=4, t=PACK)[:, us],
-                va_raw[g][:, :, cols].rearrange("p t (a b u) -> p u a t b", u=PACK, b=4)[:, us],
+                va_raw[g][h][:].rearrange("p t (a b u) -> p u a t b", u=PACK, b=4)[:, us],
             )
 
         def quantize_va(g, h):
@@ -165,13 +168,14 @@ def tile_approximate_inverse_descent_directio_k5_kernel(
         def multiply_am(g, j0, width, t):
             bank = new_bank([P, width], F32)
             am_banks[g, j0, t] = bank
-            i0 = g * HALF + t * P
+            i0 = t * P
+            m0 = j0 % HALF
             for kg in range(GROUPS):
                 nc.tensor.matmul_mx(
                     out=bank[:],
-                    lhsT=a_st[:, kg, 2 * i0 : 2 * (i0 + P)].bitcast(FP4X4),
-                    lhsT_scale=a_sc[:, kg, i0 : i0 + P],
-                    rhs=m_mv[:, kg, 2 * j0 : 2 * (j0 + width)].bitcast(FP4X4),
+                    lhsT=a_st[g][:, kg, 2 * i0 : 2 * (i0 + P)].bitcast(FP4X4),
+                    lhsT_scale=a_sc[g][:, kg, i0 : i0 + P],
+                    rhs=m_mv[j0 // HALF][:, kg, 2 * m0 : 2 * (m0 + width)].bitcast(FP4X4),
                     rhs_scale=m_sc[:, kg, j0 : j0 + width],
                     start=(kg == 0),
                     stop=(kg == GROUPS - 1),
@@ -179,7 +183,7 @@ def tile_approximate_inverse_descent_directio_k5_kernel(
 
         def residual(g, j0, width, t):
             bank = am_banks[g, j0, t][:].rearrange("p (m u e) -> p u m e", u=PACK, e=PACK)
-            row = r_rows[g][:, t, j0 : j0 + width].rearrange("p (u m e) -> p u m e", u=PACK, e=PACK)
+            row = r_rows[g, j0][:, t, :].rearrange("p (u m e) -> p u m e", u=PACK, e=PACK)
             spans = [(0, t), (t + 1, PACK)] if g == j0 // HALF else [(0, PACK)]
             for u0, u1 in spans:
                 if u1 > u0:
@@ -192,7 +196,7 @@ def tile_approximate_inverse_descent_directio_k5_kernel(
             p0 = (j0 - g * HALF) // PACK
             for t in range(PACK):
                 bank = am_banks[g, j0, t][:].rearrange("p (m u e) -> p u m e", u=PACK, e=PACK)
-                row = r_rows[g][:, t, j0 : j0 + width].rearrange("p (u m e) -> p u m e", u=PACK, e=PACK)
+                row = r_rows[g, j0][:, t, :].rearrange("p (u m e) -> p u m e", u=PACK, e=PACK)
                 nc.vector.scalar_tensor_tensor(
                     out=row[:, t],
                     in0=bank[:, t],
@@ -202,13 +206,15 @@ def tile_approximate_inverse_descent_directio_k5_kernel(
                     op1=ADD,
                 )
 
-        def interleave_r(engine, g, j0, width):
+        def interleave_r(engine, g, j0, width, part=None):
+            runs = width // (2 * PACK * PACK)
+            ms = slice(0, 2 * runs) if part is None else slice(part * runs, (part + 1) * runs)
             copy_on(
                 engine,
                 r_il[g][:, PACK * j0 : PACK * (j0 + width)].rearrange(
                     "p (m u e t) -> p u m t e", u=PACK, e=PACK, t=PACK
-                ),
-                r_rows[g][:, :, j0 : j0 + width].rearrange("p t (u m e) -> p u m t e", u=PACK, e=PACK),
+                )[:, :, ms],
+                r_rows[g, j0][:].rearrange("p t (u m e) -> p u m t e", u=PACK, e=PACK)[:, :, ms],
             )
 
         def quantize_r(g, j0, width):
@@ -218,11 +224,8 @@ def tile_approximate_inverse_descent_directio_k5_kernel(
                 in_=r_il[g][:, PACK * j0 : PACK * (j0 + width)],
             )
 
-        def halve_d(g, j0, width):
-            cols = slice(j0, j0 + width)
-            nc.vector.tensor_scalar(
-                out=d_half[g][:, :, cols], in0=d_raw[g][:, :, cols], scalar1=BETA, scalar2=None, op0=MULT
-            )
+        def halve_d(g):
+            nc.vector.tensor_scalar(out=d_half[g][:], in0=d_raw[g][:], scalar1=BETA, scalar2=None, op0=MULT)
 
         g_banks = {}
 
@@ -243,7 +246,7 @@ def tile_approximate_inverse_descent_directio_k5_kernel(
 
         def direction(g, j0, width, t):
             nc.vector.scalar_tensor_tensor(
-                out=y[g][:, t, j0 : j0 + width],
+                out=y[g, j0][:, t, :],
                 in0=g_banks[g, j0, t][:],
                 scalar=step_sb[:, g, t : t + 1],
                 in1=d_half[g][:, t, j0 : j0 + width],
@@ -253,13 +256,14 @@ def tile_approximate_inverse_descent_directio_k5_kernel(
 
         def store_y(g, j0, width, t0, t1):
             rows = out_0[g * HALF : (g + 1) * HALF, j0 : j0 + width].rearrange("(p t) n -> p t n", t=PACK)
-            nc.sync.dma_start(out=rows[:, t0:t1, :], in_=y[g][:, t0:t1, j0 : j0 + width])
+            nc.sync.dma_start(out=rows[:, t0:t1, :], in_=y[g, j0][:, t0:t1, :])
 
         def interleave_y(engine, g, j0, width):
+            base = max(j for gg, j in y if gg == g and j <= j0)
             copy_on(
                 engine,
                 y_il[g][:, PACK * j0 : PACK * (j0 + width)].rearrange("p (a b t) -> p a t b", b=4, t=PACK),
-                y[g][:, :, j0 : j0 + width].rearrange("p t (a b) -> p a t b", b=4),
+                y[g, base][:, :, j0 - base : j0 - base + width].rearrange("p t (a b) -> p a t b", b=4),
             )
 
         def quantize_y(g, j0, width):
@@ -283,6 +287,7 @@ def tile_approximate_inverse_descent_directio_k5_kernel(
                 )
 
         def stage1(g, j0, width):
+            r_rows[g, j0] = sb("r_rows%d_%d" % (g, j0), [P, PACK, width], BF16)
             for t in range(PACK):
                 multiply_am(g, j0, width, t)
                 residual(g, j0, width, t)
@@ -293,6 +298,7 @@ def tile_approximate_inverse_descent_directio_k5_kernel(
 
         def stage2_out(g, j0, width, stores):
             per_store = PACK // stores
+            y[g, j0] = sb("y%d_%d" % (g, j0), [P, PACK, width], F32)
             for t in range(PACK):
                 direction(g, j0, width, t)
                 if (t + 1) % per_store == 0:
@@ -301,84 +307,80 @@ def tile_approximate_inverse_descent_directio_k5_kernel(
         clear(a_raw_sc)
         clear(m_sc)
         clear(v_rows)
-        load_va(nc.scalar, 0, 0)
-        identity()
+        load_m(nc.sync, 0, 512)
         load_scale(nc.sync, a_raw_sc, a_scales, 0)
         load_scale(nc.sync, a_raw_sc, a_scales, 1)
         load_scale(nc.sync, a_raw_sc, a_scales, 2)
         load_scale(nc.sync, a_raw_sc, a_scales, 3)
-        load_scale(nc.gpsimd, m_sc, m_scales, 0)
-        load_scale(nc.gpsimd, m_sc, m_scales, 1)
-        load_scale(nc.gpsimd, m_sc, m_scales, 2)
-        load_scale(nc.gpsimd, m_sc, m_scales, 3)
-        neg_identity()
+        load_scale(nc.scalar, m_sc, m_scales, 0)
+        load_scale(nc.scalar, m_sc, m_scales, 1)
         load_a(nc.sync)
+        identity()
+        neg_identity()
         load_v(nc.sync)
-        load_m(nc.sync, 0, 512)
+        load_scale(nc.sync, m_sc, m_scales, 2)
+        load_scale(nc.sync, m_sc, m_scales, 3)
+        load_va(nc.sync, 0, 0)
         load_va(nc.sync, 1, 0)
-        load_step(nc.sync)
         load_va(nc.sync, 0, 1)
-        load_va(nc.sync, 1, 1)
         load_m(nc.sync, 512, 512)
-        load_d(nc.sync, 0, 0, 512)
-        load_d(nc.sync, 1, 0, 512)
-        load_d(nc.sync, 0, 512, 512)
-        load_d(nc.sync, 1, 512, 512)
-        interleave_va("V", 0, 0, 0)
-        interleave_va("S", 0, 0, 1)
-        prepare_v()
-        make_v_diag(0)
-        make_v_diag(1)
-        quantize_va(0, 0)
+        load_d(nc.sync, 0)
+        load_step(nc.sync)
+        load_va(nc.sync, 1, 1)
+        load_d(nc.sync, 1)
         permute_a(0)
+        prepare_v()
+        make_v_diag("S", 0)
         permute_a(1)
+        make_v_diag("V", 1)
         stage1(0, 0, 512)
+        interleave_va("V", 0, 0)
         interleave_va("V", 1, 0)
-        interleave_va("V", 0, 1)
-        quantize_va(1, 0)
         diag(0, 512)
-        stage1(1, 0, 512)
-        interleave_va("V", 1, 1)
-        quantize_va(0, 1)
+        interleave_va("V", 0, 1, 0)
         interleave_r("V", 0, 0, 512)
-        stage1(0, 512, 512)
-        quantize_va(1, 1)
-        interleave_r("V", 1, 0, 512)
-        halve_d(0, 0, 512)
-        quantize_r(0, 0, 512)
+        stage1(1, 0, 512)
+        interleave_va("S", 0, 1, 1)
+        quantize_va(1, 0)
+        quantize_va(0, 0)
         stage1(1, 512, 512)
-        quantize_r(1, 0, 512)
-        stage2_mm(0, 0, 512)
-        interleave_r("S", 0, 512, 512)
-        halve_d(1, 0, 512)
+        halve_d(0)
+        interleave_r("S", 1, 0, 512, 1)
+        interleave_r("V", 1, 0, 512, 0)
+        stage1(0, 512, 512)
+        quantize_r(0, 0, 512)
         diag(512, 512)
+        quantize_r(1, 0, 512)
+        interleave_va("S", 1, 1)
+        stage2_mm(0, 0, 512)
+        interleave_r("V", 1, 512, 512)
         stage2_out(0, 0, 512, 2)
+        interleave_r("S", 0, 512, 512)
+        quantize_va(0, 1)
+        quantize_va(1, 1)
         stage2_mm(1, 0, 512)
-        quantize_r(0, 512, 512)
-        interleave_r("S", 1, 512, 512)
-        stage2_out(1, 0, 512, 2)
-        interleave_y("S", 0, 0, 512)
+        halve_d(1)
         quantize_r(1, 512, 512)
-        halve_d(0, 512, 512)
-        interleave_y("S", 1, 0, 512)
-        halve_d(1, 512, 256)
-        halve_d(1, 768, 256)
+        quantize_r(0, 512, 512)
+        interleave_y("S", 0, 0, 512)
         stage2_mm(0, 512, 512)
+        stage2_out(1, 0, 512, 2)
+        stage2_mm(1, 512, 256)
         quantize_y(0, 0, 512)
         store_codes(0, 0, 512)
+        interleave_y("S", 1, 0, 512)
         stage2_out(0, 512, 512, 2)
-        quantize_y(1, 0, 512)
-        store_codes(1, 0, 512)
-        stage2_mm(1, 512, 256)
         stage2_mm(1, 768, 256)
         stage2_out(1, 512, 256, 1)
         interleave_y("S", 0, 512, 512)
+        quantize_y(1, 0, 512)
+        store_codes(1, 0, 512)
         stage2_out(1, 768, 256, 1)
         interleave_y("S", 1, 512, 256)
         quantize_y(0, 512, 512)
+        store_codes(0, 512, 512)
         interleave_y("V", 1, 768, 256)
         quantize_y(1, 512, 256)
-        store_codes(0, 512, 512)
         quantize_y(1, 768, 256)
-        store_scales(nc.scalar)
         store_codes(1, 512, 512)
+        store_scales(nc.scalar)

@@ -46,8 +46,9 @@ def tile_approximate_inverse_descent_directio_k5_kernel(
 
         ident = sb("ident", [P, P], BF16)
         neg_ident = sb("neg_ident", [P, P], BF16)
-        v_rows = sb("v_rows", [P, GROUPS, P], BF16)
-        neg_v = sb("neg_v", [P, GROUPS, PACK], F32)
+        vec_raw = sb("vec_raw", [P, HALF], BF16)
+        v_rows = sb("v_rows", [P, PACK, P], BF16)
+        neg_v = sb("neg_v", [P, PACK, GROUPS], F32)
         v_diag = sb("v_diag", [P, GROUPS, PACK, P], BF16)
         step_sb = sb("step_sb", [P, GROUPS, PACK], BF16)
         a_raw = sb("a_raw", [P, GROUPS, 2 * N], U8)
@@ -113,10 +114,7 @@ def tile_approximate_inverse_descent_directio_k5_kernel(
             )
 
         def load_v(queue):
-            queue.dma_start(
-                out=v_rows[0:PACK, :, :].rearrange("t g (m e) -> t (g m) e", e=PACK),
-                in_=v.rearrange("(m t e) -> t m e", t=PACK, e=PACK),
-            )
+            queue.dma_start(out=vec_raw[0:GROUPS, :], in_=v.rearrange("(g n) -> g n", g=GROUPS))
 
         def load_step(queue):
             queue.dma_start(out=step_sb[:], in_=step.rearrange("(g p t) -> p g t", p=P, t=PACK))
@@ -135,20 +133,24 @@ def tile_approximate_inverse_descent_directio_k5_kernel(
             )
 
         def prepare_v():
-            bank = new_bank([P, GROUPS, P], BF16)
-            for g in range(GROUPS):
-                nc.tensor.transpose(bank[:, g, :], v_rows[:, g, :], ident[:])
-            nc.scalar.activation(out=neg_v[:], in_=bank[:, :, 0:PACK], func=COPY, scale=-1.0)
+            nc.scalar.copy(
+                out=v_rows[0:GROUPS].rearrange("g t (m e) -> g t m e", e=PACK),
+                in_=vec_raw[0:GROUPS, :].rearrange("g (m t e) -> g t m e", t=PACK, e=PACK),
+            )
+            bank = new_bank([P, PACK, P], BF16)
+            for t in range(PACK):
+                nc.tensor.transpose(bank[:, t, :], v_rows[:, t, :], ident[:])
+            nc.scalar.activation(out=neg_v[:], in_=bank[:, :, 0:GROUPS], func=COPY, scale=-1.0)
 
         def make_v_diag(engine, g):
             for t in range(PACK):
                 if engine == "V":
                     nc.vector.tensor_scalar(
-                        out=v_diag[:, g, t, :], in0=neg_ident[:], scalar1=neg_v[:, g, t : t + 1], scalar2=None, op0=MULT
+                        out=v_diag[:, g, t, :], in0=neg_ident[:], scalar1=neg_v[:, t, g : g + 1], scalar2=None, op0=MULT
                     )
                 else:
                     nc.scalar.activation(
-                        out=v_diag[:, g, t, :], in_=neg_ident[:], func=COPY, scale=neg_v[:, g, t : t + 1]
+                        out=v_diag[:, g, t, :], in_=neg_ident[:], func=COPY, scale=neg_v[:, t, g : g + 1]
                     )
 
         def interleave_va(engine, g, h, part=None):
@@ -188,7 +190,7 @@ def tile_approximate_inverse_descent_directio_k5_kernel(
             for u0, u1 in spans:
                 if u1 > u0:
                     nc.scalar.activation(
-                        out=row[:, u0:u1], in_=bank[:, u0:u1], func=COPY, scale=neg_v[:, g, t : t + 1]
+                        out=row[:, u0:u1], in_=bank[:, u0:u1], func=COPY, scale=neg_v[:, t, g : g + 1]
                     )
 
         def diag(j0, width):
@@ -200,7 +202,7 @@ def tile_approximate_inverse_descent_directio_k5_kernel(
                 nc.vector.scalar_tensor_tensor(
                     out=row[:, t],
                     in0=bank[:, t],
-                    scalar=neg_v[:, g, t : t + 1],
+                    scalar=neg_v[:, t, g : g + 1],
                     in1=v_diag[:, g, t, p0 : p0 + width // PACK].rearrange("p (m e) -> p m e", e=PACK),
                     op0=MULT,
                     op1=ADD,
@@ -307,48 +309,48 @@ def tile_approximate_inverse_descent_directio_k5_kernel(
         clear(a_raw_sc)
         clear(m_sc)
         clear(v_rows)
+        load_v(nc.scalar)
         load_m(nc.sync, 0, 512)
         load_scale(nc.sync, a_raw_sc, a_scales, 0)
         load_scale(nc.sync, a_raw_sc, a_scales, 1)
         load_scale(nc.sync, a_raw_sc, a_scales, 2)
         load_scale(nc.sync, a_raw_sc, a_scales, 3)
         load_scale(nc.scalar, m_sc, m_scales, 0)
-        load_scale(nc.scalar, m_sc, m_scales, 1)
         load_a(nc.sync)
         identity()
         neg_identity()
-        load_v(nc.sync)
+        load_scale(nc.sync, m_sc, m_scales, 1)
         load_scale(nc.sync, m_sc, m_scales, 2)
         load_scale(nc.sync, m_sc, m_scales, 3)
         load_va(nc.sync, 0, 0)
         load_va(nc.sync, 1, 0)
         load_va(nc.sync, 0, 1)
         load_m(nc.sync, 512, 512)
+        load_va(nc.sync, 1, 1)
         load_d(nc.sync, 0)
         load_step(nc.sync)
-        load_va(nc.sync, 1, 1)
         load_d(nc.sync, 1)
         permute_a(0)
         prepare_v()
         make_v_diag("S", 0)
         permute_a(1)
         make_v_diag("V", 1)
-        stage1(0, 0, 512)
         interleave_va("V", 0, 0)
+        stage1(0, 0, 512)
         interleave_va("V", 1, 0)
+        interleave_va("S", 0, 1, 1)
         diag(0, 512)
         interleave_va("V", 0, 1, 0)
         interleave_r("V", 0, 0, 512)
         stage1(1, 0, 512)
-        interleave_va("S", 0, 1, 1)
         quantize_va(1, 0)
         quantize_va(0, 0)
         stage1(1, 512, 512)
         halve_d(0)
         interleave_r("S", 1, 0, 512, 1)
-        interleave_r("V", 1, 0, 512, 0)
-        stage1(0, 512, 512)
         quantize_r(0, 0, 512)
+        stage1(0, 512, 512)
+        interleave_r("V", 1, 0, 512, 0)
         diag(512, 512)
         quantize_r(1, 0, 512)
         interleave_va("S", 1, 1)
@@ -358,8 +360,8 @@ def tile_approximate_inverse_descent_directio_k5_kernel(
         interleave_r("S", 0, 512, 512)
         quantize_va(0, 1)
         quantize_va(1, 1)
-        stage2_mm(1, 0, 512)
         halve_d(1)
+        stage2_mm(1, 0, 512)
         quantize_r(1, 512, 512)
         quantize_r(0, 512, 512)
         interleave_y("S", 0, 0, 512)
@@ -371,8 +373,8 @@ def tile_approximate_inverse_descent_directio_k5_kernel(
         interleave_y("S", 1, 0, 512)
         stage2_out(0, 512, 512, 2)
         stage2_mm(1, 768, 256)
-        stage2_out(1, 512, 256, 1)
         interleave_y("S", 0, 512, 512)
+        stage2_out(1, 512, 256, 1)
         quantize_y(1, 0, 512)
         store_codes(1, 0, 512)
         stage2_out(1, 768, 256, 1)

@@ -330,48 +330,51 @@ def tile_approximate_inverse_descent_directio_k5_kernel(
         load_d(nc.sync, 0)
         load_step(nc.sync)
         load_d(nc.sync, 1)
-        permute_a(0)
         prepare_v()
         make_v_diag("S", 0)
-        permute_a(1)
+        permute_a(0)
         make_v_diag("V", 1)
-        interleave_va("V", 0, 0)
+        permute_a(1)
+        interleave_va("V", 0, 0, 0)
+        interleave_va("S", 0, 0, 1)
+        quantize_va(0, 0)
         stage1(0, 0, 512)
         interleave_va("V", 1, 0)
-        interleave_va("S", 0, 1, 1)
         diag(0, 512)
-        interleave_va("V", 0, 1, 0)
-        interleave_r("V", 0, 0, 512)
         stage1(1, 0, 512)
+        interleave_va("S", 0, 1, 1)
         quantize_va(1, 0)
-        quantize_va(0, 0)
-        stage1(1, 512, 512)
-        halve_d(0)
+        interleave_r("V", 0, 0, 512)
         interleave_r("S", 1, 0, 512, 1)
+        stage1(1, 512, 512)
+        interleave_va("V", 1, 1, 1)
         quantize_r(0, 0, 512)
         stage1(0, 512, 512)
         interleave_r("V", 1, 0, 512, 0)
-        diag(512, 512)
+        interleave_va("V", 0, 1, 0)
         quantize_r(1, 0, 512)
-        interleave_va("S", 1, 1)
-        stage2_mm(0, 0, 512)
-        interleave_r("V", 1, 512, 512)
-        stage2_out(0, 0, 512, 2)
-        interleave_r("S", 0, 512, 512)
+        interleave_va("S", 1, 1, 0)
+        halve_d(0)
+        diag(512, 512)
         quantize_va(0, 1)
+        stage2_mm(0, 0, 512)
+        interleave_r("V", 1, 512, 512, 1)
+        interleave_r("S", 0, 512, 512)
+        stage2_out(0, 0, 512, 2)
         quantize_va(1, 1)
         halve_d(1)
         stage2_mm(1, 0, 512)
-        quantize_r(1, 512, 512)
+        interleave_r("S", 1, 512, 512, 0)
         quantize_r(0, 512, 512)
-        interleave_y("S", 0, 0, 512)
-        stage2_mm(0, 512, 512)
         stage2_out(1, 0, 512, 2)
-        stage2_mm(1, 512, 256)
+        interleave_y("S", 0, 0, 512)
+        quantize_r(1, 512, 512)
         quantize_y(0, 0, 512)
-        store_codes(0, 0, 512)
+        stage2_mm(0, 512, 512)
         interleave_y("S", 1, 0, 512)
+        store_codes(0, 0, 512)
         stage2_out(0, 512, 512, 2)
+        stage2_mm(1, 512, 256)
         stage2_mm(1, 768, 256)
         interleave_y("S", 0, 512, 512)
         stage2_out(1, 512, 256, 1)
@@ -379,10 +382,10 @@ def tile_approximate_inverse_descent_directio_k5_kernel(
         store_codes(1, 0, 512)
         stage2_out(1, 768, 256, 1)
         interleave_y("S", 1, 512, 256)
+        interleave_y("V", 1, 768, 256)
         quantize_y(0, 512, 512)
         store_codes(0, 512, 512)
-        interleave_y("V", 1, 768, 256)
-        quantize_y(1, 512, 256)
         quantize_y(1, 768, 256)
+        quantize_y(1, 512, 256)
         store_codes(1, 512, 512)
         store_scales(nc.scalar)

from contextlib import ExitStack

import concourse.mybir as mybir
from concourse.masks import make_identity

N = 1024
FLOPS = 2 * 2 * N * N * N

F32 = mybir.dt.float32
BF16 = mybir.dt.bfloat16
I32 = mybir.dt.int32
U32 = mybir.dt.uint32
U8 = mybir.dt.uint8
FP8X4 = mybir.dt.float8_e4m3fn_x4
FP4X4 = mybir.dt.float4_e2m1fn_x4
COPY = mybir.ActivationFunctionType.Copy
MULT = mybir.AluOpType.mult
ADD = mybir.AluOpType.add

P = 128
PACK = 4
HALF = 512
GROUPS = N // HALF
BANKS = 8
BETA = 0.5


def tile_approximate_inverse_descent_directio_k5_kernel(
    tc, a_words, a_scales, m_words, m_scales, va, v, step, d_prev, out_0, out_1, out_2
):
    nc = tc.nc
    with ExitStack() as ctx:
        keep = ctx.enter_context(tc.tile_pool(name="keep", bufs=1))
        psum = ctx.enter_context(tc.psum_pool(name="psum", bufs=1))
        ctx.enter_context(tc.manual_schedule())

        def sb(name, shape, dtype):
            return keep.tile(shape, dtype, name=name, align_bytes=64)

        bank_count = [0]

        def new_bank(shape, dtype):
            k = bank_count[0] % BANKS
            bank_count[0] += 1
            return psum.tile(shape, dtype, name="bank%d" % k)

        ident = sb("ident", [P, P], BF16)
        neg_ident = sb("neg_ident", [P, P], BF16)
        vec_raw = sb("vec_raw", [P, HALF], BF16)
        v_rows = sb("v_rows", [P, PACK, P], BF16)
        neg_v = sb("neg_v", [P, PACK, GROUPS], F32)
        v_diag = sb("v_diag", [P, GROUPS, PACK, P], BF16)
        step_sb = sb("step_sb", [P, GROUPS, PACK], BF16)
        a_raw = sb("a_raw", [P, GROUPS, 2 * N], U8)
        a_raw_sc = sb("a_raw_sc", [P, GROUPS, N], U8)
        a_st = [sb("a_st%d" % g, [P, GROUPS, 2 * HALF], U8) for g in range(GROUPS)]
        a_sc = [sb("a_sc%d" % g, [P, GROUPS, HALF], U8) for g in range(GROUPS)]
        m_mv = [sb("m_mv%d" % h, [P, GROUPS, 2 * HALF], U8) for h in range(GROUPS)]
        m_sc = sb("m_sc", [P, GROUPS, N], U8)
        va_raw = [[sb("va_raw%d%d" % (g, h), [P, PACK, HALF], BF16) for h in range(GROUPS)] for g in range(GROUPS)]
        va_il = [[sb("va_il%d%d" % (g, h), [P, PACK * HALF], BF16) for h in range(GROUPS)] for g in range(GROUPS)]
        va_codes = sb("va_codes", [P, GROUPS, N], U32)
        va_sc = sb("va_sc", [P, GROUPS, N], U8)
        r_rows = {}
        r_il = [sb("r_il%d" % g, [P, N * PACK], BF16) for g in range(GROUPS)]
        r_codes = sb("r_codes", [P, GROUPS, N], U32)
        r_sc = sb("r_sc", [P, GROUPS, N], U8)
        d_raw = [sb("d_raw%d" % g, [P, PACK, N], BF16) for g in range(GROUPS)]
        d_half = [sb("d_half%d" % g, [P, PACK, N], BF16) for g in range(GROUPS)]
        y = {}
        y_il = [sb("y_il%d" % g, [P, N * PACK], BF16) for g in range(GROUPS)]
        y_codes = sb("y_codes", [P, GROUPS, N], U32)
        y_sc = sb("y_sc", [P, GROUPS, N], U8)

        def copy_on(engine, out, in_):
            if engine == "V":
                nc.vector.tensor_copy(out=out, in_=in_)
            else:
                nc.scalar.copy(out=out, in_=in_)

        def load_va(queue, g, h):
            cols = slice(h * HALF, (h + 1) * HALF)
            rows = va[g * HALF : (g + 1) * HALF, cols].rearrange("(m t e) c -> e m t c", t=PACK, e=PACK)
            for e in range(PACK):
                queue.dma_start(out=va_raw[g][h][e:P:PACK, :, :], in_=rows[e])

        def load_scale(queue, plane, scales, q):
            queue.dma_start(
                out=plane[32 * q : 32 * q + 4, :, :].bitcast(I32),
                in_=scales[:, 4 * q : 4 * q + 4, :].rearrange("g r n -> r g n").bitcast(I32),
            )

        def load_d(queue, g):
            queue.dma_start(
                out=d_raw[g][:], in_=d_prev[g * HALF : (g + 1) * HALF, :].rearrange("(p t) n -> p t n", t=PACK)
            )

        def clear(plane):
            nc.vector.memset(plane[:].bitcast(I32), 0)

        def identity():
            make_identity(nc, ident[:])

        def neg_identity():
            nc.scalar.activation(out=neg_ident[:], in_=ident[:], func=COPY, scale=-1.0)

        def load_a(queue):
            queue.dma_start(out=a_raw[:].bitcast(I32), in_=a_words.rearrange("g p n -> p g n").bitcast(I32))

        def load_m(queue, j0, width):
            cols = slice(2 * j0, 2 * (j0 + width))
            queue.dma_start(
                out=m_mv[j0 // HALF][:].bitcast(I32), in_=m_words[:, :, cols].rearrange("g p n -> p g n").bitcast(I32)
            )

        def load_v(queue):
            queue.dma_start(out=vec_raw[0:GROUPS, :], in_=v.rearrange("(g n) -> g n", g=GROUPS))

        def load_step(queue):
            queue.dma_start(out=step_sb[:], in_=step.rearrange("(g p t) -> p g t", p=P, t=PACK))

        def permute_a(g):
            nc.vector.tensor_copy(
                out=a_st[g][:].bitcast(I32).rearrange("p k (t m w) -> p k t m w", t=PACK, w=2),
                in_=a_raw[:, :, 2 * g * HALF : 2 * (g + 1) * HALF]
                .bitcast(I32)
                .rearrange("p k (m t w) -> p k t m w", t=PACK, w=2),
            )
            cols = slice(g * HALF, (g + 1) * HALF)
            nc.vector.tensor_copy(
                out=a_sc[g][:].bitcast(I32).rearrange("p k (t m) -> p k t m", t=PACK),
                in_=a_raw_sc[:, :, cols].bitcast(I32).rearrange("p k (m t) -> p k t m", t=PACK),
            )

        def prepare_v():
            nc.scalar.copy(
                out=v_rows[0:GROUPS].rearrange("g t (m e) -> g t m e", e=PACK),
                in_=vec_raw[0:GROUPS, :].rearrange("g (m t e) -> g t m e", t=PACK, e=PACK),
            )
            bank = new_bank([P, PACK, P], BF16)
            for t in range(PACK):
                nc.tensor.transpose(bank[:, t, :], v_rows[:, t, :], ident[:])
            nc.scalar.activation(out=neg_v[:], in_=bank[:, :, 0:GROUPS], func=COPY, scale=-1.0)

        def make_v_diag(engine, g):
            for t in range(PACK):
                if engine == "V":
                    nc.vector.tensor_scalar(
                        out=v_diag[:, g, t, :], in0=neg_ident[:], scalar1=neg_v[:, t, g : g + 1], scalar2=None, op0=MULT
                    )
                else:
                    nc.scalar.activation(
                        out=v_diag[:, g, t, :], in_=neg_ident[:], func=COPY, scale=neg_v[:, t, g : g + 1]
                    )

        def interleave_va(engine, g, h, part=None):
            us = slice(0, PACK) if part is None else slice(2 * part, 2 * part + 2)
            copy_on(
                engine,
                va_il[g][h][:].rearrange("p (u a b t) -> p u a t b", u=PACK, b=4, t=PACK)[:, us],
                va_raw[g][h][:].rearrange("p t (a b u) -> p u a t b", u=PACK, b=4)[:, us],
            )

        def quantize_va(g, h):
            cols = slice(h * HALF, (h + 1) * HALF)
            nc.vector.quantize_mx(out=va_codes[:, g, cols].bitcast(FP8X4), scales=va_sc[:, g, cols], in_=va_il[g][h][:])

        am_banks = {}

        def multiply_am(g, j0, width, t):
            bank = new_bank([P, width], F32)
            am_banks[g, j0, t] = bank
            i0 = t * P
            m0 = j0 % HALF
            for kg in range(GROUPS):
                nc.tensor.matmul_mx(
                    out=bank[:],
                    lhsT=a_st[g][:, kg, 2 * i0 : 2 * (i0 + P)].bitcast(FP4X4),
                    lhsT_scale=a_sc[g][:, kg, i0 : i0 + P],
                    rhs=m_mv[j0 // HALF][:, kg, 2 * m0 : 2 * (m0 + width)].bitcast(FP4X4),
                    rhs_scale=m_sc[:, kg, j0 : j0 + width],
                    start=(kg == 0),
                    stop=(kg == GROUPS - 1),
                )

        def residual(g, j0, width, t):
            bank = am_banks[g, j0, t][:].rearrange("p (m u e) -> p u m e", u=PACK, e=PACK)
            row = r_rows[g, j0][:, t, :].rearrange("p (u m e) -> p u m e", u=PACK, e=PACK)
            spans = [(0, t), (t + 1, PACK)] if g == j0 // HALF else [(0, PACK)]
            for u0, u1 in spans:
                if u1 > u0:
                    nc.scalar.activation(
                        out=row[:, u0:u1], in_=bank[:, u0:u1], func=COPY, scale=neg_v[:, t, g : g + 1]
                    )

        def diag(j0, width):
            g = j0 // HALF
            p0 = (j0 - g * HALF) // PACK
            for t in range(PACK):
                bank = am_banks[g, j0, t][:].rearrange("p (m u e) -> p u m e", u=PACK, e=PACK)
                row = r_rows[g, j0][:, t, :].rearrange("p (u m e) -> p u m e", u=PACK, e=PACK)
                nc.vector.scalar_tensor_tensor(
                    out=row[:, t],
                    in0=bank[:, t],
                    scalar=neg_v[:, t, g : g + 1],
                    in1=v_diag[:, g, t, p0 : p0 + width // PACK].rearrange("p (m e) -> p m e", e=PACK),
                    op0=MULT,
                    op1=ADD,
                )

        def interleave_r(engine, g, j0, width, part=None):
            runs = width // (2 * PACK * PACK)
            ms = slice(0, 2 * runs) if part is None else slice(part * runs, (part + 1) * runs)
            copy_on(
                engine,
                r_il[g][:, PACK * j0 : PACK * (j0 + width)].rearrange(
                    "p (m u e t) -> p u m t e", u=PACK, e=PACK, t=PACK
                )[:, :, ms],
                r_rows[g, j0][:].rearrange("p t (u m e) -> p u m t e", u=PACK, e=PACK)[:, :, ms],
            )

        def quantize_r(g, j0, width):
            nc.vector.quantize_mx(
                out=r_codes[:, g, j0 : j0 + width].bitcast(FP8X4),
                scales=r_sc[:, g, j0 : j0 + width],
                in_=r_il[g][:, PACK * j0 : PACK * (j0 + width)],
            )

        def halve_d(g):
            nc.vector.tensor_scalar(out=d_half[g][:], in0=d_raw[g][:], scalar1=BETA, scalar2=None, op0=MULT)

        g_banks = {}

        def multiply_g(g, j0, width, t):
            bank = new_bank([P, width], F32)
            g_banks[g, j0, t] = bank
            c0 = g * HALF + t * P
            for kg in range(GROUPS):
                nc.tensor.matmul_mx(
                    out=bank[:],
                    lhsT=va_codes[:, kg, c0 : c0 + P].bitcast(FP8X4),
                    lhsT_scale=va_sc[:, kg, c0 : c0 + P],
                    rhs=r_codes[:, kg, j0 : j0 + width].bitcast(FP8X4),
                    rhs_scale=r_sc[:, kg, j0 : j0 + width],
                    start=(kg == 0),
                    stop=(kg == GROUPS - 1),
                )

        def direction(g, j0, width, t):
            nc.vector.scalar_tensor_tensor(
                out=y[g, j0][:, t, :],
                in0=g_banks[g, j0, t][:],
                scalar=step_sb[:, g, t : t + 1],
                in1=d_half[g][:, t, j0 : j0 + width],
                op0=MULT,
                op1=ADD,
            )

        def store_y(g, j0, width, t0, t1):
            rows = out_0[g * HALF : (g + 1) * HALF, j0 : j0 + width].rearrange("(p t) n -> p t n", t=PACK)
            nc.sync.dma_start(out=rows[:, t0:t1, :], in_=y[g, j0][:, t0:t1, :])

        def interleave_y(engine, g, j0, width):
            base = max(j for gg, j in y if gg == g and j <= j0)
            copy_on(
                engine,
                y_il[g][:, PACK * j0 : PACK * (j0 + width)].rearrange("p (a b t) -> p a t b", b=4, t=PACK),
                y[g, base][:, :, j0 - base : j0 - base + width].rearrange("p t (a b) -> p a t b", b=4),
            )

        def quantize_y(g, j0, width):
            nc.vector.quantize_mx(
                out=y_codes[:, g, j0 : j0 + width].bitcast(FP8X4),
                scales=y_sc[:, g, j0 : j0 + width],
                in_=y_il[g][:, PACK * j0 : PACK * (j0 + width)],
            )

        def store_codes(g, j0, width):
            nc.sync.dma_start(
                out=out_1[g].rearrange("p n t -> p (n t)")[:, PACK * j0 : PACK * (j0 + width)].bitcast(I32),
                in_=y_codes[:, g, j0 : j0 + width].bitcast(I32),
            )

        def store_scales(queue):
            for q in range(4):
                queue.dma_start(
                    out=out_2[:, 4 * q : 4 * q + 4, :].rearrange("g r n -> r g n").bitcast(I32),
                    in_=y_sc[32 * q : 32 * q + 4, :, :].bitcast(I32),
                )

        def stage1(g, j0, width):
            r_rows[g, j0] = sb("r_rows%d_%d" % (g, j0), [P, PACK, width], BF16)
            for t in range(PACK):
                multiply_am(g, j0, width, t)
                residual(g, j0, width, t)

        def stage2_mm(g, j0, width):
            for t in range(PACK):
                multiply_g(g, j0, width, t)

        def stage2_out(g, j0, width, stores):
            per_store = PACK // stores
            y[g, j0] = sb("y%d_%d" % (g, j0), [P, PACK, width], F32)
            for t in range(PACK):
                direction(g, j0, width, t)
                if (t + 1) % per_store == 0:
                    store_y(g, j0, width, t + 1 - per_store, t + 1)

        clear(a_raw_sc)
        clear(m_sc)
        clear(v_rows)
        load_v(nc.scalar)
        load_m(nc.sync, 0, 512)
        load_scale(nc.sync, a_raw_sc, a_scales, 0)
        load_scale(nc.sync, a_raw_sc, a_scales, 1)
        load_scale(nc.sync, a_raw_sc, a_scales, 2)
        load_scale(nc.sync, a_raw_sc, a_scales, 3)
        load_scale(nc.scalar, m_sc, m_scales, 0)
        load_a(nc.sync)
        identity()
        neg_identity()
        load_scale(nc.sync, m_sc, m_scales, 1)
        load_scale(nc.sync, m_sc, m_scales, 2)
        load_scale(nc.sync, m_sc, m_scales, 3)
        load_va(nc.sync, 0, 0)
        load_va(nc.sync, 1, 0)
        load_va(nc.sync, 0, 1)
        load_m(nc.sync, 512, 512)
        load_va(nc.sync, 1, 1)
        load_d(nc.sync, 0)
        load_step(nc.sync)
        load_d(nc.sync, 1)
        prepare_v()
        make_v_diag("S", 0)
        permute_a(0)
        make_v_diag("V", 1)
        permute_a(1)
        interleave_va("V", 0, 0, 0)
        interleave_va("S", 0, 0, 1)
        quantize_va(0, 0)
        stage1(0, 0, 512)
        interleave_va("V", 1, 0)
        diag(0, 512)
        stage1(1, 0, 512)
        interleave_va("S", 0, 1, 1)
        quantize_va(1, 0)
        interleave_r("V", 0, 0, 512)
        interleave_r("S", 1, 0, 512, 1)
        stage1(1, 512, 512)
        interleave_va("V", 1, 1, 1)
        quantize_r(0, 0, 512)
        stage1(0, 512, 512)
        interleave_r("V", 1, 0, 512, 0)
        interleave_va("V", 0, 1, 0)
        quantize_r(1, 0, 512)
        interleave_va("S", 1, 1, 0)
        halve_d(0)
        diag(512, 512)
        quantize_va(0, 1)
        stage2_mm(0, 0, 512)
        interleave_r("V", 1, 512, 512, 1)
        interleave_r("S", 0, 512, 512)
        stage2_out(0, 0, 512, 2)
        quantize_va(1, 1)
        halve_d(1)
        stage2_mm(1, 0, 512)
        interleave_r("S", 1, 512, 512, 0)
        quantize_r(0, 512, 512)
        stage2_out(1, 0, 512, 2)
        interleave_y("S", 0, 0, 512)
        quantize_r(1, 512, 512)
        quantize_y(0, 0, 512)
        stage2_mm(0, 512, 512)
        interleave_y("S", 1, 0, 512)
        store_codes(0, 0, 512)
        stage2_out(0, 512, 512, 2)
        stage2_mm(1, 512, 256)
        stage2_mm(1, 768, 256)
        interleave_y("S", 0, 512, 512)
        stage2_out(1, 512, 256, 1)
        quantize_y(1, 0, 512)
        store_codes(1, 0, 512)
        stage2_out(1, 768, 256, 1)
        interleave_y("S", 1, 512, 256)
        interleave_y("V", 1, 768, 256)
        quantize_y(0, 512, 512)
        store_codes(0, 512, 512)
        quantize_y(1, 768, 256)
        quantize_y(1, 512, 256)
        store_codes(1, 512, 512)
        store_scales(nc.scalar)
